import numpy as np, ml_dtypes
CORES = [0,1,2,3,4,5,6,7]
N = 8
def setup_inputs(rng):
    return {"x1": rng.standard_normal((N, 128, 4), dtype=np.float32), "x2": rng.standard_normal((N, 128, 256), dtype=np.float32).astype(ml_dtypes.bfloat16)}
def reference(x1, x2):
    out = []
    s = x1.sum(axis=0, dtype=np.float64).astype(x1.dtype)
    out.append(np.broadcast_to(s, (N,) + s.shape))
    g = np.concatenate(list(x2), axis=1)
    out.append(np.broadcast_to(g, (N,) + g.shape))
    return {"y1": out[0], "y2": out[1]}

from concourse.bass import DstId, RemoteDMATransfer

N = 8
W1 = 4
W2 = 256

SCRATCH = {
    "g1": ("sbuf", [128, N * W1], "float32"),
    "s1": ("sbuf", [128, W1], "float32"),
    "g2": ("sbuf", [128, N * W2], "bfloat16"),
}
SEMAPHORES = ["ld1", "ld2", "arr1", "sum1", "arr2", "sent", "st"]

M1 = 0xC000
E1 = 2
X2_SPLIT = ((0x00FF, 8, 4), (0x0F00, 4, 2), (0x3000, 2, 1))


def rank_program(g, core, T, topo):
    rank = T.rank_of(core)
    if rank is None:
        return
    cores = list(T.cores)

    def dst_id(c):
        rid, pid, sengine = topo.addr(c)
        return DstId(rid=rid, pnc=pid)

    roots = []
    for d in sorted(set(topo.die(c) for c in cores)):
        roots.append([c for c in cores if topo.die(c) == d][0])
    is_root = core in roots

    slot1 = T.g1[:, rank * W1:(rank + 1) * W1]
    block2 = T.g2[:, rank * W2:(rank + 1) * W2]

    g.dma_start(slot1, T.x1[:]).then_inc(T.sem.ld1, 16)
    g.dma_start(block2, T.x2[:]).then_inc(T.sem.ld2, 16)
    sent = 0

    to = [c for c in roots if c != core]
    g.wait_ge(T.sem.ld1, 16)
    g.remote_dma_fused(
        [RemoteDMATransfer(dst_ids=[dst_id(c) for c in to], dma_engine_mask=M1, remote_sem=T.sem.arr1,
                           srcs=[slot1], dsts=[slot1 for c in to], alu_op=0)],
        local_sem=T.sem.sent)
    sent += E1

    g.wait_ge(T.sem.ld2, 16)
    transfers = []
    step = 1
    for mask, engines, ndst in X2_SPLIT:
        to = [cores[(rank + step + k) % N] for k in range(ndst)]
        step += ndst
        transfers.append(RemoteDMATransfer(dst_ids=[dst_id(c) for c in to], dma_engine_mask=mask,
                                           remote_sem=T.sem.arr2, srcs=[block2], dsts=[block2 for c in to],
                                           alu_op=0))
        sent += engines
    g.remote_dma_fused(transfers, local_sem=T.sem.sent)

    if is_root:
        to = [c for c in cores if c != core and (topo.die(c) == topo.die(core) or c in roots)]
        g.wait_ge(T.sem.arr1, (N - 1) * E1)
        g.remote_dma_fused(
            [RemoteDMATransfer(dst_ids=[dst_id(c) for c in to], dma_engine_mask=M1, remote_sem=T.sem.sum1,
                               srcs=[T.g1[:, j * W1:(j + 1) * W1] for j in range(N)],
                               dsts=[T.s1[:] for c in to], alu_op=1)],
            local_sem=T.sem.sent)
        sent += E1

    g.wait_ge(T.sem.sum1, E1)
    g.dma_start(T.y1[:], T.s1[:]).then_inc(T.sem.st, 16)

    g.wait_ge(T.sem.arr2, sum(e * n for m, e, n in X2_SPLIT))
    g.dma_start(T.y2[:], T.g2[:]).then_inc(T.sem.st, 16)

    g.wait_ge(T.sem.st, 32)
    g.wait_ge(T.sem.sent, sent)
